import numpy as np
import ml_dtypes


def mxq(x, axis, fmt="e4m3"):
    dtype, down = {"e4m3": (ml_dtypes.float8_e4m3fn, 7), "e5m2": (ml_dtypes.float8_e5m2, 14)}[fmt]
    v = np.moveaxis(np.asarray(x, np.float32).astype(ml_dtypes.bfloat16).astype(np.float64), axis, -1)
    blocks = v.reshape(v.shape[:-1] + (-1, 32))
    amax = np.abs(blocks).max(-1, keepdims=True)
    byte = np.maximum(np.where(amax > 0, np.frexp(amax)[1] - 1 + 127, 0) - down, 1)
    scale = np.exp2(byte - 127.0)
    codes = (blocks / scale).astype(np.float32).astype(dtype).astype(np.float64)
    return np.moveaxis((codes * scale).reshape(v.shape), -1, axis)


WIDE = False


def mx_kscale(k):
    if not WIDE:
        return np.ones(k)
    levels = np.array([10, -10, 5, -5, 0])
    if k % 512:
        return np.exp2(np.random.permutation(np.resize(levels, k // 32))).repeat(32)
    a = np.empty((k // 512, 16))
    for p in range(k // 512):
        a[p, :8] = np.random.permutation(np.resize(levels, 8))
        for g in range(8):
            far = levels[np.abs(levels - a[p, g]) >= 10]
            a[p, g + 8] = far[np.random.randint(len(far))]
    return np.exp2(a.ravel()).repeat(32)


def f64(x):
    return np.asarray(x).astype(np.float64)


def striped8(idx):
    return np.asarray(idx).reshape(8, -1, 16).transpose(0, 2, 1).reshape(128, -1).astype(np.uint16)


def unstriped8(offs):
    return offs.reshape(8, 16, -1).transpose(0, 2, 1).reshape(8, -1).astype(np.int64)


def pick8(x, idx, run):
    r = np.arange(len(x))
    return x[r[:, None], idx[r % (8 * run) // run]]


E2M1 = np.array([0.0, 0.5, 1.0, 1.5, 2.0, 3.0, 4.0, 6.0, -0.0, -0.5, -1.0, -1.5, -2.0, -3.0, -4.0, -6.0])


def pack_weight(w, fmt):
    k, n = w.shape
    w = f64(np.asarray(w, np.float32).astype(ml_dtypes.bfloat16)).reshape(k // 32, 32, n)
    amax = np.abs(w).max(1)
    if fmt == "e4m3":
        byte = np.frexp(amax)[1] - 1 + 127 - 7
    else:
        mant, ex = np.frexp(amax / 6.0)
        byte = np.where(mant > 0.5, ex, ex - 1) + 127
    byte = np.clip(np.where(amax > 0, byte, 1), 1, 254)
    scaled = (w * np.exp2(127.0 - byte)[:, None, :]).reshape(k, n).astype(np.float32)
    by_word = np.ascontiguousarray(scaled.reshape(k // 512, 128, 4, n).transpose(0, 1, 3, 2))
    if fmt == "e4m3":
        words = by_word.astype(ml_dtypes.float8_e4m3fn).view(np.uint8)
    else:
        c = by_word.astype(ml_dtypes.float4_e2m1fn).view(np.uint8) & 0xF
        words = (c[..., 0::2] | (c[..., 1::2] << 4)).reshape(k // 512, 128, 2 * n)
    return np.ascontiguousarray(words), np.ascontiguousarray(byte.astype(np.uint8).reshape(k // 512, 16, n))


def unpack_weight(words, scales, fmt):
    g, _, n = scales.shape
    words = np.ascontiguousarray(words).reshape(g, 128, n, -1)
    if fmt == "e4m3":
        vals = words.view(ml_dtypes.float8_e4m3fn).astype(np.float64)
    else:
        nib = np.empty((g, 128, n, 4), np.uint8)
        nib[..., 0::2] = words & 0xF
        nib[..., 1::2] = words >> 4
        vals = E2M1[nib]
    vals = vals * np.repeat(np.exp2(scales.astype(np.float64) - 127.0), 8, axis=1)[..., None]
    return vals.transpose(0, 1, 3, 2).reshape(g * 512, n)


def softplus(v):
    return np.log(1.0 + np.exp(v))


D, T, I, Q = 512, 1024, 512, 128


def setup_inputs():
    n = np.random.standard_normal
    idx = np.stack([np.random.permutation(T)[:I] for _ in range(8)])
    idx2 = np.stack([np.random.permutation(T)[:I] for _ in range(8)])
    idx4 = np.stack([np.random.permutation(T)[:I] for _ in range(8)])
    fd = mx_kscale(D)
    keysp = pack_weight(n((D, T)) / fd[:, None], "e2m1")
    return {
        "query": (n((D, Q)) * 0.9 / np.sqrt(D) * fd[:, None]).astype(np.float32),
        "query2": (n((D, Q)) * 0.9 / np.sqrt(D) * fd[:, None]).astype(np.float32),
        "keys_words": keysp[0],
        "keys_scales": keysp[1],
        "lam": (np.random.uniform(0.6, 1.2, (Q, 1))).astype(np.float32),
        "lean": (np.random.uniform(0.2, 0.6, (Q, 1))).astype(np.float32),
        "old": (np.random.uniform(0.0, 2.0, (Q, T))).astype(np.float32),
        "gainm": (np.random.uniform(0.5, 1.5, (Q, I))).astype(np.float32),
        "offs": striped8(idx),
        "offs2": striped8(idx2),
        "offs4": striped8(idx4),
    }


def reference(query, query2, keys_words, keys_scales, lam, lean, old, gainm, offs, offs2, offs4):
    idx = unstriped8(offs)
    idx2 = unstriped8(offs2)
    idx4 = unstriped8(offs4)
    keysu = unpack_weight(keys_words, keys_scales, "e2m1")
    queryq = mxq(f64(query), 0, "e4m3")
    a = queryq.T @ keysu
    query2q = mxq(f64(query2), 0, "e4m3")
    b = query2q.T @ keysu
    s = pick8(a, idx, 16) / (softplus(pick8(b, idx2, 16)) + 0.5) * f64(lam)
    p = np.exp(s - np.max(s, axis=1, keepdims=True))
    r = p / np.sum(p, axis=1, keepdims=True)
    m0 = np.sum(r * s, axis=1, keepdims=True)
    dv0 = np.square(s - m0)
    v0 = np.sum(r * dv0, axis=1, keepdims=True)
    w = r * ((dv0 - v0) * f64(lean) + 1.0)
    ws = w * f64(gainm) * 256.0
    wf = np.zeros((Q, T))
    wf[np.arange(Q)[:, None], idx4[np.arange(Q) % 128 // 16]] = ws
    y = f64(old) + wf
    return y

@@ -1,0 +1,227 @@
+import math
+from contextlib import ExitStack
+
+import concourse.mybir as mybir
+
+D, T, I, Q = 512, 1024, 512, 128
+FLOPS = 2 * 2 * D * T * Q
+
+F32 = mybir.dt.float32
+BF16 = mybir.dt.bfloat16
+I32 = mybir.dt.int32
+U32 = mybir.dt.uint32
+U16 = mybir.dt.uint16
+U8 = mybir.dt.uint8
+FP8X4 = mybir.dt.float8_e4m3fn_x4
+FP4X4 = mybir.dt.float4_e2m1fn_x4
+ALU = mybir.AluOpType
+ACT = mybir.ActivationFunctionType
+
+P = 128
+PACK = 4
+HALF = I // 2
+B_N = 256
+A_N = 512
+SCALAR_SLOTS = 320
+EXP_CAP = 2.0**60
+OUT_CHUNK = 256
+
+
+def tile_attend_worthfor_varyleaning_moved_heads_kernel(
+    tc, query, query2, keys_words, keys_scales, lam, lean, old, gainm, offs, offs2, offs4, out
+):
+    nc = tc.nc
+    with ExitStack() as ctx:
+        sb = ctx.enter_context(tc.tile_pool(name="sb", bufs=1))
+        ps = ctx.enter_context(tc.psum_pool(name="ps", bufs=1))
+
+        def column(name):
+            return sb.tile([P, 1], F32, name=name)
+
+        def slots(name):
+            return sb.tile([P, I], F32, name=name)
+
+        key_scale = sb.tile([P, T], U8, name="key_scale", align_bytes=64)
+        ones = column("ones")
+        nc.vector.memset(ones[:], 1.0)
+
+        q2_raw = sb.tile([P, PACK * Q], F32, name="q2_raw", tag="slot_q2")
+        nc.sync.dma_start(out=q2_raw[:], in_=query2.rearrange("(p j) w -> p (j w)", j=PACK))
+        for quad in range(4):
+            nc.scalar.dma_start(
+                out=key_scale[32 * quad : 32 * quad + 4, :].bitcast(I32),
+                in_=keys_scales[0, 4 * quad : 4 * quad + 4, :].bitcast(I32),
+            )
+        key_words = sb.tile([P, 2 * T], U8, name="key_words", tag="slot_keys", align_bytes=64)
+        nc.sync.dma_start(out=key_words[:], in_=keys_words[0])
+        q_raw = sb.tile([P, PACK * Q], F32, name="q_raw", tag="slot_q")
+        nc.sync.dma_start(out=q_raw[:], in_=query.rearrange("(p j) w -> p (j w)", j=PACK))
+        list_b = sb.tile([P, I // 16], U16, name="list_b")
+        nc.sync.dma_start(list_b[:], offs2)
+        list_a = sb.tile([P, I // 16], U16, name="list_a")
+        nc.sync.dma_start(list_a[:], offs)
+        list_out = sb.tile([P, I // 16], U16, name="list_out")
+        nc.sync.dma_start(list_out[:], offs4)
+
+        root_e = column("root_e")
+        nc.scalar.activation(root_e[:], ones[:], ACT.Copy, scale=math.exp(0.5))
+
+        placed = sb.tile([P, T], F32, name="placed")
+        nc.vector.memset(placed[:], 0.0)
+        lam_col = column("lam_col")
+        nc.gpsimd.dma_start(out=lam_col[:], in_=lam)
+        lean_col = column("lean_col")
+        nc.gpsimd.dma_start(out=lean_col[:], in_=lean)
+        signs = sb.tile([P, 3], F32, name="signs")
+        nc.vector.memset(signs[:, 1:2], -1.0)
+        nc.vector.memset(signs[:, 2:3], 1.0)
+
+        def quantise(raw, name):
+            grouped = sb.tile([P, Q * PACK], BF16, name=name + "_grouped", align_bytes=64)
+            nc.vector.tensor_copy(
+                out=grouped[:].rearrange("p (c i t) -> p c t i", i=4, t=PACK),
+                in_=raw[:].rearrange("p (t c i) -> p c t i", i=4, t=PACK),
+            )
+            codes = sb.tile([P, Q], U32, name=name + "_codes", align_bytes=64)
+            scale = sb.tile([P, Q], U8, name=name + "_scale", align_bytes=64)
+            nc.vector.quantize_mx(out=codes[:].bitcast(FP8X4), scales=scale[:], in_=grouped[:])
+            return codes, scale
+
+        def score(codes, scale, first, width, name):
+            bank = ps.tile([P, width], F32, name=name)
+            nc.tensor.matmul_mx(
+                out=bank[:],
+                lhsT=codes[:].bitcast(FP8X4),
+                lhsT_scale=scale[:],
+                rhs=key_words[:, 2 * first : 2 * (first + width)].bitcast(FP4X4),
+                rhs_scale=key_scale[:, first : first + width],
+                start=True,
+                stop=True,
+            )
+            return bank
+
+        q2_codes, q2_scale = quantise(q2_raw, "q2")
+        q_codes, q_scale = quantise(q_raw, "q")
+
+        gain = sb.tile([P, I], F32, name="gain", tag="slot_q2")
+        nc.sync.dma_start(out=gain[:], in_=gainm)
+        old_lo = sb.tile([P, T // 2], F32, name="old_lo", tag="slot_q")
+        nc.sync.dma_start(out=old_lo[:], in_=old[:, : T // 2])
+
+        b_all = sb.tile([P, T], F32, name="b_all")
+        for c in range(T // B_N):
+            bank = score(q2_codes, q2_scale, c * B_N, B_N, "b_bank%d" % c)
+            cols = slice(c * B_N, (c + 1) * B_N)
+            if c < T // B_N - 1:
+                nc.scalar.copy(b_all[:, cols], bank[:])
+            else:
+                nc.vector.tensor_copy(b_all[:, cols], bank[:])
+        a_banks = [score(q_codes, q_scale, c * A_N, A_N, "a_bank%d" % c) for c in range(T // A_N)]
+        old_hi = sb.tile([P, T // 2], F32, name="old_hi", tag="slot_keys", align_bytes=64)
+        nc.sync.dma_start(out=old_hi[:], in_=old[:, T // 2 :])
+
+        halves = [slice(0, HALF), slice(HALF, I)]
+        list_halves = [slice(0, HALF // 16), slice(HALF // 16, I // 16)]
+        by_scalar = slice(0, SCALAR_SLOTS)
+        by_vector = slice(SCALAR_SLOTS, I)
+        neg_lam = column("neg_lam")
+        nc.scalar.activation(neg_lam[:], lam_col[:], ACT.Copy, scale=-1.0)
+        b_picked = slots("b_picked")
+        grown = slots("grown")
+        nc.scalar.activation(grown[:, halves[1]], b_all[:].indirect(list_b[:, list_halves[1]]), ACT.Exp)
+        nc.vector.tensor_copy(b_picked[:, halves[0]], b_all[:].indirect(list_b[:, list_halves[0]]))
+        nc.scalar.activation(grown[:, halves[0]], b_picked[:, halves[0]], ACT.Exp)
+        nc.vector.tensor_copy(b_picked[:, halves[1]], b_all[:].indirect(list_b[:, list_halves[1]]))
+        capped = slots("capped")
+        for h in (halves[1], halves[0]):
+            nc.vector.tensor_scalar_min(capped[:, h], grown[:, h], EXP_CAP)
+        floor = sb.tile([P, SCALAR_SLOTS], F32, name="floor")
+        nc.vector.tensor_scalar(floor[:], b_picked[:, by_scalar], 0.5, 0.5, ALU.add, ALU.max)
+        a_all = sb.tile([P, T], F32, name="a_all")
+        for c in range(T // A_N):
+            nc.vector.tensor_copy(a_all[:, c * A_N : (c + 1) * A_N], a_banks[c][:])
+        a_picked = sb.tile([P, SCALAR_SLOTS], F32, name="a_picked")
+        nc.vector.tensor_copy(a_picked[:], a_all[:].indirect(list_a[:, : SCALAR_SLOTS // 16]))
+
+        soft = slots("soft")
+        for part in (by_vector, by_scalar):
+            nc.scalar.activation(soft[:, part], capped[:, part], ACT.Ln, bias=root_e[:], scale=math.exp(0.5))
+        log_floor = sb.tile([P, SCALAR_SLOTS], F32, name="log_floor")
+        nc.scalar.activation(log_floor[:], floor[:], ACT.Ln)
+        log_soft = sb.tile([P, SCALAR_SLOTS], F32, name="log_soft")
+        nc.scalar.activation(log_soft[:], soft[:, by_scalar], ACT.Ln)
+        den = sb.tile([P, I - SCALAR_SLOTS], F32, name="den")
+        nc.vector.scalar_tensor_tensor(den[:], b_picked[:, by_vector], 0.5, soft[:, by_vector], ALU.add, ALU.max)
+        log_den = sb.tile([P, SCALAR_SLOTS], F32, name="log_den")
+        nc.vector.tensor_tensor(log_den[:], log_soft[:], log_floor[:], ALU.max)
+        inv_den = slots("inv_den")
+        nc.vector.reciprocal(inv_den[:, by_vector], den[:])
+        nc.scalar.activation(inv_den[:, by_scalar], log_den[:], ACT.Exp, scale=-1.0)
+
+        ratio = slots("ratio")
+        neg_s = slots("neg_s")
+        neg_max_part = column("neg_max_part")
+        neg_max = column("neg_max")
+        nc.vector.tensor_tensor(
+            ratio[:, by_vector], a_all[:].indirect(list_a[:, SCALAR_SLOTS // 16 :]), inv_den[:, by_vector], ALU.mult
+        )
+        nc.vector.tensor_scalar(
+            neg_s[:, by_vector], ratio[:, by_vector], neg_lam[:], None, ALU.mult, ALU.min, accum_out=neg_max_part[:]
+        )
+        nc.vector.tensor_tensor(ratio[:, by_scalar], a_picked[:], inv_den[:, by_scalar], ALU.mult)
+        nc.vector.tensor_scalar(
+            neg_s[:, by_scalar], ratio[:, by_scalar], neg_lam[:], neg_max_part[:], ALU.mult, ALU.min,
+            accum_out=neg_max[:],
+        )
+
+        p = slots("p")
+        sums = sb.tile([P, 3], F32, name="sums")
+        neg_first, second, total = sums[:, 0:1], sums[:, 1:2], sums[:, 2:3]
+        nc.scalar.activation(p[:], neg_s[:], ACT.Exp, bias=neg_max[:], scale=-1.0, accum_out=total)
+        depth = slots("depth")
+        nc.vector.tensor_scalar(depth[:], neg_s[:], neg_max[:], None, ALU.subtract)
+        depth_sq = slots("depth_sq")
+        nc.scalar.activation(depth_sq[:], depth[:], ACT.Square)
+
+        inv_total = column("inv_total")
+        nc.vector.reciprocal(inv_total[:], total)
+        first_terms = slots("first_terms")
+        nc.vector.scalar_tensor_tensor(
+            first_terms[:], depth[:], -1.0, p[:], ALU.mult, ALU.mult, accum_out=neg_first
+        )
+        second_terms = slots("second_terms")
+        nc.vector.scalar_tensor_tensor(
+            second_terms[:], depth_sq[:], lean_col[:], p[:], ALU.mult, ALU.mult, accum_out=second
+        )
+
+        out_scale = column("out_scale")
+        lean_once = column("lean_once")
+        lean_twice = column("lean_twice")
+        nc.scalar.activation(lean_once[:], inv_total[:], ACT.Copy, scale=lean_col[:])
+        nc.scalar.activation(out_scale[:], inv_total[:], ACT.Copy, scale=256.0)
+        nc.scalar.activation(signs[:, 0:1], neg_first, ACT.Copy, scale=lean_once[:])
+        dev_sq = slots("dev_sq")
+        nc.scalar.activation(dev_sq[:], depth[:], ACT.Square, bias=neg_first, scale=total)
+        nc.scalar.activation(lean_twice[:], lean_once[:], ACT.Copy, scale=inv_total[:])
+
+        offset_terms = sb.tile([P, 3], F32, name="offset_terms")
+        offset = column("offset")
+        nc.vector.scalar_tensor_tensor(
+            offset_terms[:], sums[:], inv_total[:], signs[:], ALU.mult, ALU.mult, accum_out=offset[:]
+        )
+        leaning = slots("leaning")
+        nc.vector.tensor_scalar(leaning[:], dev_sq[:], lean_twice[:], offset[:], ALU.mult, ALU.add)
+        share = slots("share")
+        for h in halves:
+            nc.vector.scalar_tensor_tensor(share[:, h], p[:, h], out_scale[:], gain[:, h], ALU.mult, ALU.mult)
+
+        nc.vector.tensor_tensor(placed[:].indirect(list_out[:]), share[:], leaning[:], ALU.mult)
+
+        result = sb.tile([P, T], F32, name="result")
+        for c in range(T // OUT_CHUNK):
+            cols = slice(c * OUT_CHUNK, (c + 1) * OUT_CHUNK)
+            src = old_lo if c * OUT_CHUNK < T // 2 else old_hi
+            lo = c * OUT_CHUNK % (T // 2)
+            nc.vector.tensor_tensor(result[:, cols], placed[:, cols], src[:, lo : lo + OUT_CHUNK], ALU.add)
+            queue = nc.sync if c % 2 == 0 else nc.scalar
+            queue.dma_start(out=out[:, cols], in_=result[:, cols])

@@ -20,11 +20,11 @@ ACT = mybir.ActivationFunctionType
 P = 128
 PACK = 4
 HALF = I // 2
-B_N = 256
+B_WIDTHS = (256, 256, 256, 128, 128)
 A_N = 512
 SCALAR_SLOTS = 320
 EXP_CAP = 2.0**60
-OUT_CHUNK = 256
+OUT_WIDTHS = (192, 320, 320, 192)
 
 
 def tile_attend_worthfor_varyleaning_moved_heads_kernel(
@@ -69,9 +69,9 @@ def tile_attend_worthfor_varyleaning_moved_heads_kernel(
         placed = sb.tile([P, T], F32, name="placed")
         nc.vector.memset(placed[:], 0.0)
         lam_col = column("lam_col")
-        nc.gpsimd.dma_start(out=lam_col[:], in_=lam)
+        nc.sync.dma_start(out=lam_col[:], in_=lam)
         lean_col = column("lean_col")
-        nc.gpsimd.dma_start(out=lean_col[:], in_=lean)
+        nc.sync.dma_start(out=lean_col[:], in_=lean)
         signs = sb.tile([P, 3], F32, name="signs")
         nc.vector.memset(signs[:, 1:2], -1.0)
         nc.vector.memset(signs[:, 2:3], 1.0)
@@ -109,13 +109,14 @@ def tile_attend_worthfor_varyleaning_moved_heads_kernel(
         nc.sync.dma_start(out=old_lo[:], in_=old[:, : T // 2])
 
         b_all = sb.tile([P, T], F32, name="b_all")
-        for c in range(T // B_N):
-            bank = score(q2_codes, q2_scale, c * B_N, B_N, "b_bank%d" % c)
-            cols = slice(c * B_N, (c + 1) * B_N)
-            if c < T // B_N - 1:
-                nc.scalar.copy(b_all[:, cols], bank[:])
+        first = 0
+        for c, width in enumerate(B_WIDTHS):
+            bank = score(q2_codes, q2_scale, first, width, "b_bank%d" % c)
+            if width == B_WIDTHS[0]:
+                nc.scalar.copy(b_all[:, first : first + width], bank[:])
             else:
-                nc.vector.tensor_copy(b_all[:, cols], bank[:])
+                nc.vector.tensor_copy(b_all[:, first : first + width], bank[:])
+            first = first + width
         a_banks = [score(q_codes, q_scale, c * A_N, A_N, "a_bank%d" % c) for c in range(T // A_N)]
         old_hi = sb.tile([P, T // 2], F32, name="old_hi", tag="slot_keys", align_bytes=64)
         nc.sync.dma_start(out=old_hi[:], in_=old[:, T // 2 :])
@@ -124,19 +125,23 @@ def tile_attend_worthfor_varyleaning_moved_heads_kernel(
         list_halves = [slice(0, HALF // 16), slice(HALF // 16, I // 16)]
         by_scalar = slice(0, SCALAR_SLOTS)
         by_vector = slice(SCALAR_SLOTS, I)
-        neg_lam = column("neg_lam")
-        nc.scalar.activation(neg_lam[:], lam_col[:], ACT.Copy, scale=-1.0)
-        b_picked = slots("b_picked")
+        neg_lifted = slots("neg_lifted")
+
+        def pick_b(k):
+            nc.vector.tensor_scalar(
+                neg_lifted[:, halves[k]], b_all[:].indirect(list_b[:, list_halves[k]]), -1.0, -0.5, ALU.mult, ALU.add
+            )
+
         grown = slots("grown")
         nc.scalar.activation(grown[:, halves[1]], b_all[:].indirect(list_b[:, list_halves[1]]), ACT.Exp)
-        nc.vector.tensor_copy(b_picked[:, halves[0]], b_all[:].indirect(list_b[:, list_halves[0]]))
-        nc.scalar.activation(grown[:, halves[0]], b_picked[:, halves[0]], ACT.Exp)
-        nc.vector.tensor_copy(b_picked[:, halves[1]], b_all[:].indirect(list_b[:, list_halves[1]]))
+        pick_b(0)
+        nc.scalar.activation(grown[:, halves[0]], neg_lifted[:, halves[0]], ACT.Exp, bias=-0.5, scale=-1.0)
+        pick_b(1)
         capped = slots("capped")
         for h in (halves[1], halves[0]):
             nc.vector.tensor_scalar_min(capped[:, h], grown[:, h], EXP_CAP)
         floor = sb.tile([P, SCALAR_SLOTS], F32, name="floor")
-        nc.vector.tensor_scalar(floor[:], b_picked[:, by_scalar], 0.5, 0.5, ALU.add, ALU.max)
+        nc.vector.tensor_scalar(floor[:], neg_lifted[:, by_scalar], -1.0, 0.5, ALU.mult, ALU.max)
         a_all = sb.tile([P, T], F32, name="a_all")
         for c in range(T // A_N):
             nc.vector.tensor_copy(a_all[:, c * A_N : (c + 1) * A_N], a_banks[c][:])
@@ -151,7 +156,7 @@ def tile_attend_worthfor_varyleaning_moved_heads_kernel(
         log_soft = sb.tile([P, SCALAR_SLOTS], F32, name="log_soft")
         nc.scalar.activation(log_soft[:], soft[:, by_scalar], ACT.Ln)
         den = sb.tile([P, I - SCALAR_SLOTS], F32, name="den")
-        nc.vector.scalar_tensor_tensor(den[:], b_picked[:, by_vector], 0.5, soft[:, by_vector], ALU.add, ALU.max)
+        nc.vector.scalar_tensor_tensor(den[:], soft[:, by_vector], -1.0, neg_lifted[:, by_vector], ALU.mult, ALU.min)
         log_den = sb.tile([P, SCALAR_SLOTS], F32, name="log_den")
         nc.vector.tensor_tensor(log_den[:], log_soft[:], log_floor[:], ALU.max)
         inv_den = slots("inv_den")
@@ -166,11 +171,11 @@ def tile_attend_worthfor_varyleaning_moved_heads_kernel(
             ratio[:, by_vector], a_all[:].indirect(list_a[:, SCALAR_SLOTS // 16 :]), inv_den[:, by_vector], ALU.mult
         )
         nc.vector.tensor_scalar(
-            neg_s[:, by_vector], ratio[:, by_vector], neg_lam[:], None, ALU.mult, ALU.min, accum_out=neg_max_part[:]
+            neg_s[:, by_vector], ratio[:, by_vector], lam_col[:], None, ALU.mult, ALU.min, accum_out=neg_max_part[:]
         )
-        nc.vector.tensor_tensor(ratio[:, by_scalar], a_picked[:], inv_den[:, by_scalar], ALU.mult)
+        nc.vector.scalar_tensor_tensor(ratio[:, by_scalar], a_picked[:], -1.0, inv_den[:, by_scalar], ALU.mult, ALU.mult)
         nc.vector.tensor_scalar(
-            neg_s[:, by_scalar], ratio[:, by_scalar], neg_lam[:], neg_max_part[:], ALU.mult, ALU.min,
+            neg_s[:, by_scalar], ratio[:, by_scalar], lam_col[:], neg_max_part[:], ALU.mult, ALU.min,
             accum_out=neg_max[:],
         )
 
@@ -210,7 +215,12 @@ def tile_attend_worthfor_varyleaning_moved_heads_kernel(
             offset_terms[:], sums[:], inv_total[:], signs[:], ALU.mult, ALU.mult, accum_out=offset[:]
         )
         leaning = slots("leaning")
-        nc.vector.tensor_scalar(leaning[:], dev_sq[:], lean_twice[:], offset[:], ALU.mult, ALU.add)
+        nc.scalar.activation(
+            leaning[:, by_vector], dev_sq[:, by_vector], ACT.Identity, bias=offset[:], scale=lean_twice[:]
+        )
+        nc.vector.tensor_scalar(
+            leaning[:, by_scalar], dev_sq[:, by_scalar], lean_twice[:], offset[:], ALU.mult, ALU.add
+        )
         share = slots("share")
         for h in halves:
             nc.vector.scalar_tensor_tensor(share[:, h], p[:, h], out_scale[:], gain[:, h], ALU.mult, ALU.mult)
@@ -218,10 +228,12 @@ def tile_attend_worthfor_varyleaning_moved_heads_kernel(
         nc.vector.tensor_tensor(placed[:].indirect(list_out[:]), share[:], leaning[:], ALU.mult)
 
         result = sb.tile([P, T], F32, name="result")
-        for c in range(T // OUT_CHUNK):
-            cols = slice(c * OUT_CHUNK, (c + 1) * OUT_CHUNK)
-            src = old_lo if c * OUT_CHUNK < T // 2 else old_hi
-            lo = c * OUT_CHUNK % (T // 2)
-            nc.vector.tensor_tensor(result[:, cols], placed[:, cols], src[:, lo : lo + OUT_CHUNK], ALU.add)
+        first = 0
+        for c, width in enumerate(OUT_WIDTHS):
+            cols = slice(first, first + width)
+            src = old_lo if first < T // 2 else old_hi
+            lo = first % (T // 2)
+            nc.vector.tensor_tensor(result[:, cols], placed[:, cols], src[:, lo : lo + width], ALU.add)
             queue = nc.sync if c % 2 == 0 else nc.scalar
             queue.dma_start(out=out[:, cols], in_=result[:, cols])
+            first = first + width

@@ -48,7 +48,8 @@ def tile_attend_worthfor_varyleaning_moved_heads_kernel(
         q2_raw = sb.tile([P, PACK * Q], F32, name="q2_raw", tag="slot_q2")
         nc.sync.dma_start(out=q2_raw[:], in_=query2.rearrange("(p j) w -> p (j w)", j=PACK))
         for quad in range(4):
-            nc.scalar.dma_start(
+            queue = nc.sync if quad < 2 else nc.scalar
+            queue.dma_start(
                 out=key_scale[32 * quad : 32 * quad + 4, :].bitcast(I32),
                 in_=keys_scales[0, 4 * quad : 4 * quad + 4, :].bitcast(I32),
             )
@@ -161,7 +162,9 @@ def tile_attend_worthfor_varyleaning_moved_heads_kernel(
         nc.vector.tensor_tensor(log_den[:], log_soft[:], log_floor[:], ALU.max)
         inv_den = slots("inv_den")
         nc.vector.reciprocal(inv_den[:, by_vector], den[:])
-        nc.scalar.activation(inv_den[:, by_scalar], log_den[:], ACT.Exp, scale=-1.0)
+        pieces = (slice(0, SCALAR_SLOTS // 2), slice(SCALAR_SLOTS // 2, SCALAR_SLOTS))
+        for part in pieces:
+            nc.scalar.activation(inv_den[:, part], log_den[:, part], ACT.Exp, scale=-1.0)
 
         ratio = slots("ratio")
         neg_s = slots("neg_s")
@@ -173,7 +176,8 @@ def tile_attend_worthfor_varyleaning_moved_heads_kernel(
         nc.vector.tensor_scalar(
             neg_s[:, by_vector], ratio[:, by_vector], lam_col[:], None, ALU.mult, ALU.min, accum_out=neg_max_part[:]
         )
-        nc.vector.scalar_tensor_tensor(ratio[:, by_scalar], a_picked[:], -1.0, inv_den[:, by_scalar], ALU.mult, ALU.mult)
+        for part in pieces:
+            nc.vector.scalar_tensor_tensor(ratio[:, part], a_picked[:, part], -1.0, inv_den[:, part], ALU.mult, ALU.mult)
         nc.vector.tensor_scalar(
             neg_s[:, by_scalar], ratio[:, by_scalar], lam_col[:], neg_max_part[:], ALU.mult, ALU.min,
             accum_out=neg_max[:],

import math
from contextlib import ExitStack

import concourse.mybir as mybir

D, T, I, Q = 512, 1024, 512, 128
FLOPS = 2 * 2 * D * T * Q

F32 = mybir.dt.float32
BF16 = mybir.dt.bfloat16
I32 = mybir.dt.int32
U32 = mybir.dt.uint32
U16 = mybir.dt.uint16
U8 = mybir.dt.uint8
FP8X4 = mybir.dt.float8_e4m3fn_x4
FP4X4 = mybir.dt.float4_e2m1fn_x4
ALU = mybir.AluOpType
ACT = mybir.ActivationFunctionType

P = 128
PACK = 4
HALF = I // 2
B_WIDTHS = (256, 256, 256, 128, 128)
A_N = 512
SCALAR_SLOTS = 320
EXP_CAP = 2.0**60
OUT_WIDTHS = (192, 320, 320, 192)


def tile_attend_worthfor_varyleaning_moved_heads_kernel(
    tc, query, query2, keys_words, keys_scales, lam, lean, old, gainm, offs, offs2, offs4, out
):
    nc = tc.nc
    with ExitStack() as ctx:
        sb = ctx.enter_context(tc.tile_pool(name="sb", bufs=1))
        ps = ctx.enter_context(tc.psum_pool(name="ps", bufs=1))

        def column(name):
            return sb.tile([P, 1], F32, name=name)

        def slots(name):
            return sb.tile([P, I], F32, name=name)

        key_scale = sb.tile([P, T], U8, name="key_scale", align_bytes=64)
        ones = column("ones")
        nc.vector.memset(ones[:], 1.0)

        q2_raw = sb.tile([P, PACK * Q], F32, name="q2_raw", tag="slot_q2")
        nc.sync.dma_start(out=q2_raw[:], in_=query2.rearrange("(p j) w -> p (j w)", j=PACK))
        for quad in range(4):
            queue = nc.sync if quad < 2 else nc.scalar
            queue.dma_start(
                out=key_scale[32 * quad : 32 * quad + 4, :].bitcast(I32),
                in_=keys_scales[0, 4 * quad : 4 * quad + 4, :].bitcast(I32),
            )
        key_words = sb.tile([P, 2 * T], U8, name="key_words", tag="slot_keys", align_bytes=64)
        nc.sync.dma_start(out=key_words[:], in_=keys_words[0])
        q_raw = sb.tile([P, PACK * Q], F32, name="q_raw", tag="slot_q")
        nc.sync.dma_start(out=q_raw[:], in_=query.rearrange("(p j) w -> p (j w)", j=PACK))
        list_b = sb.tile([P, I // 16], U16, name="list_b")
        nc.sync.dma_start(list_b[:], offs2)
        list_a = sb.tile([P, I // 16], U16, name="list_a")
        nc.sync.dma_start(list_a[:], offs)
        list_out = sb.tile([P, I // 16], U16, name="list_out")
        nc.sync.dma_start(list_out[:], offs4)

        root_e = column("root_e")
        nc.scalar.activation(root_e[:], ones[:], ACT.Copy, scale=math.exp(0.5))

        placed = sb.tile([P, T], F32, name="placed")
        nc.vector.memset(placed[:], 0.0)
        lam_col = column("lam_col")
        nc.sync.dma_start(out=lam_col[:], in_=lam)
        lean_col = column("lean_col")
        nc.sync.dma_start(out=lean_col[:], in_=lean)
        signs = sb.tile([P, 3], F32, name="signs")
        nc.vector.memset(signs[:, 1:2], -1.0)
        nc.vector.memset(signs[:, 2:3], 1.0)

        def quantise(raw, name):
            grouped = sb.tile([P, Q * PACK], BF16, name=name + "_grouped", align_bytes=64)
            nc.vector.tensor_copy(
                out=grouped[:].rearrange("p (c i t) -> p c t i", i=4, t=PACK),
                in_=raw[:].rearrange("p (t c i) -> p c t i", i=4, t=PACK),
            )
            codes = sb.tile([P, Q], U32, name=name + "_codes", align_bytes=64)
            scale = sb.tile([P, Q], U8, name=name + "_scale", align_bytes=64)
            nc.vector.quantize_mx(out=codes[:].bitcast(FP8X4), scales=scale[:], in_=grouped[:])
            return codes, scale

        def score(codes, scale, first, width, name):
            bank = ps.tile([P, width], F32, name=name)
            nc.tensor.matmul_mx(
                out=bank[:],
                lhsT=codes[:].bitcast(FP8X4),
                lhsT_scale=scale[:],
                rhs=key_words[:, 2 * first : 2 * (first + width)].bitcast(FP4X4),
                rhs_scale=key_scale[:, first : first + width],
                start=True,
                stop=True,
            )
            return bank

        q2_codes, q2_scale = quantise(q2_raw, "q2")
        q_codes, q_scale = quantise(q_raw, "q")

        gain = sb.tile([P, I], F32, name="gain", tag="slot_q2")
        nc.sync.dma_start(out=gain[:], in_=gainm)
        old_lo = sb.tile([P, T // 2], F32, name="old_lo", tag="slot_q")
        nc.sync.dma_start(out=old_lo[:], in_=old[:, : T // 2])

        b_all = sb.tile([P, T], F32, name="b_all")
        first = 0
        for c, width in enumerate(B_WIDTHS):
            bank = score(q2_codes, q2_scale, first, width, "b_bank%d" % c)
            if width == B_WIDTHS[0]:
                nc.scalar.copy(b_all[:, first : first + width], bank[:])
            else:
                nc.vector.tensor_copy(b_all[:, first : first + width], bank[:])
            first = first + width
        a_banks = [score(q_codes, q_scale, c * A_N, A_N, "a_bank%d" % c) for c in range(T // A_N)]
        old_hi = sb.tile([P, T // 2], F32, name="old_hi", tag="slot_keys", align_bytes=64)
        nc.sync.dma_start(out=old_hi[:], in_=old[:, T // 2 :])

        halves = [slice(0, HALF), slice(HALF, I)]
        list_halves = [slice(0, HALF // 16), slice(HALF // 16, I // 16)]
        by_scalar = slice(0, SCALAR_SLOTS)
        by_vector = slice(SCALAR_SLOTS, I)
        neg_lifted = slots("neg_lifted")

        def pick_b(k):
            nc.vector.tensor_scalar(
                neg_lifted[:, halves[k]], b_all[:].indirect(list_b[:, list_halves[k]]), -1.0, -0.5, ALU.mult, ALU.add
            )

        grown = slots("grown")
        nc.scalar.activation(grown[:, halves[1]], b_all[:].indirect(list_b[:, list_halves[1]]), ACT.Exp)
        pick_b(0)
        nc.scalar.activation(grown[:, halves[0]], neg_lifted[:, halves[0]], ACT.Exp, bias=-0.5, scale=-1.0)
        pick_b(1)
        capped = slots("capped")
        for h in (halves[1], halves[0]):
            nc.vector.tensor_scalar_min(capped[:, h], grown[:, h], EXP_CAP)
        floor = sb.tile([P, SCALAR_SLOTS], F32, name="floor")
        nc.vector.tensor_scalar(floor[:], neg_lifted[:, by_scalar], -1.0, 0.5, ALU.mult, ALU.max)
        a_all = sb.tile([P, T], F32, name="a_all")
        for c in range(T // A_N):
            nc.vector.tensor_copy(a_all[:, c * A_N : (c + 1) * A_N], a_banks[c][:])
        a_picked = sb.tile([P, SCALAR_SLOTS], F32, name="a_picked")
        nc.vector.tensor_copy(a_picked[:], a_all[:].indirect(list_a[:, : SCALAR_SLOTS // 16]))

        soft = slots("soft")
        for part in (by_vector, by_scalar):
            nc.scalar.activation(soft[:, part], capped[:, part], ACT.Ln, bias=root_e[:], scale=math.exp(0.5))
        log_floor = sb.tile([P, SCALAR_SLOTS], F32, name="log_floor")
        nc.scalar.activation(log_floor[:], floor[:], ACT.Ln)
        log_soft = sb.tile([P, SCALAR_SLOTS], F32, name="log_soft")
        nc.scalar.activation(log_soft[:], soft[:, by_scalar], ACT.Ln)
        den = sb.tile([P, I - SCALAR_SLOTS], F32, name="den")
        nc.vector.scalar_tensor_tensor(den[:], soft[:, by_vector], -1.0, neg_lifted[:, by_vector], ALU.mult, ALU.min)
        log_den = sb.tile([P, SCALAR_SLOTS], F32, name="log_den")
        nc.vector.tensor_tensor(log_den[:], log_soft[:], log_floor[:], ALU.max)
        inv_den = slots("inv_den")
        nc.vector.reciprocal(inv_den[:, by_vector], den[:])
        pieces = (slice(0, SCALAR_SLOTS // 2), slice(SCALAR_SLOTS // 2, SCALAR_SLOTS))
        for part in pieces:
            nc.scalar.activation(inv_den[:, part], log_den[:, part], ACT.Exp, scale=-1.0)

        ratio = slots("ratio")
        neg_s = slots("neg_s")
        neg_max_part = column("neg_max_part")
        neg_max = column("neg_max")
        nc.vector.tensor_tensor(
            ratio[:, by_vector], a_all[:].indirect(list_a[:, SCALAR_SLOTS // 16 :]), inv_den[:, by_vector], ALU.mult
        )
        nc.vector.tensor_scalar(
            neg_s[:, by_vector], ratio[:, by_vector], lam_col[:], None, ALU.mult, ALU.min, accum_out=neg_max_part[:]
        )
        for part in pieces:
            nc.vector.scalar_tensor_tensor(ratio[:, part], a_picked[:, part], -1.0, inv_den[:, part], ALU.mult, ALU.mult)
        nc.vector.tensor_scalar(
            neg_s[:, by_scalar], ratio[:, by_scalar], lam_col[:], neg_max_part[:], ALU.mult, ALU.min,
            accum_out=neg_max[:],
        )

        p = slots("p")
        sums = sb.tile([P, 3], F32, name="sums")
        neg_first, second, total = sums[:, 0:1], sums[:, 1:2], sums[:, 2:3]
        nc.scalar.activation(p[:], neg_s[:], ACT.Exp, bias=neg_max[:], scale=-1.0, accum_out=total)
        depth = slots("depth")
        nc.vector.tensor_scalar(depth[:], neg_s[:], neg_max[:], None, ALU.subtract)
        depth_sq = slots("depth_sq")
        nc.scalar.activation(depth_sq[:], depth[:], ACT.Square)

        inv_total = column("inv_total")
        nc.vector.reciprocal(inv_total[:], total)
        first_terms = slots("first_terms")
        nc.vector.scalar_tensor_tensor(
            first_terms[:], depth[:], -1.0, p[:], ALU.mult, ALU.mult, accum_out=neg_first
        )
        second_terms = slots("second_terms")
        nc.vector.scalar_tensor_tensor(
            second_terms[:], depth_sq[:], lean_col[:], p[:], ALU.mult, ALU.mult, accum_out=second
        )

        out_scale = column("out_scale")
        lean_once = column("lean_once")
        lean_twice = column("lean_twice")
        nc.scalar.activation(lean_once[:], inv_total[:], ACT.Copy, scale=lean_col[:])
        nc.scalar.activation(out_scale[:], inv_total[:], ACT.Copy, scale=256.0)
        nc.scalar.activation(signs[:, 0:1], neg_first, ACT.Copy, scale=lean_once[:])
        dev_sq = slots("dev_sq")
        nc.scalar.activation(dev_sq[:], depth[:], ACT.Square, bias=neg_first, scale=total)
        nc.scalar.activation(lean_twice[:], lean_once[:], ACT.Copy, scale=inv_total[:])

        offset_terms = sb.tile([P, 3], F32, name="offset_terms")
        offset = column("offset")
        nc.vector.scalar_tensor_tensor(
            offset_terms[:], sums[:], inv_total[:], signs[:], ALU.mult, ALU.mult, accum_out=offset[:]
        )
        leaning = slots("leaning")
        nc.scalar.activation(
            leaning[:, by_vector], dev_sq[:, by_vector], ACT.Identity, bias=offset[:], scale=lean_twice[:]
        )
        nc.vector.tensor_scalar(
            leaning[:, by_scalar], dev_sq[:, by_scalar], lean_twice[:], offset[:], ALU.mult, ALU.add
        )
        share = slots("share")
        for h in halves:
            nc.vector.scalar_tensor_tensor(share[:, h], p[:, h], out_scale[:], gain[:, h], ALU.mult, ALU.mult)

        nc.vector.tensor_tensor(placed[:].indirect(list_out[:]), share[:], leaning[:], ALU.mult)

        result = sb.tile([P, T], F32, name="result")
        first = 0
        for c, width in enumerate(OUT_WIDTHS):
            cols = slice(first, first + width)
            src = old_lo if first < T // 2 else old_hi
            lo = first % (T // 2)
            nc.vector.tensor_tensor(result[:, cols], placed[:, cols], src[:, lo : lo + width], ALU.add)
            queue = nc.sync if c % 2 == 0 else nc.scalar
            queue.dma_start(out=out[:, cols], in_=result[:, cols])
            first = first + width
